import numpy as np
import ml_dtypes


def mxq(x, axis, fmt="e4m3"):
    dtype, down = {"e4m3": (ml_dtypes.float8_e4m3fn, 7), "e5m2": (ml_dtypes.float8_e5m2, 14)}[fmt]
    v = np.moveaxis(np.asarray(x, np.float32).astype(ml_dtypes.bfloat16).astype(np.float64), axis, -1)
    blocks = v.reshape(v.shape[:-1] + (-1, 32))
    amax = np.abs(blocks).max(-1, keepdims=True)
    byte = np.maximum(np.where(amax > 0, np.frexp(amax)[1] - 1 + 127, 0) - down, 1)
    scale = np.exp2(byte - 127.0)
    codes = (blocks / scale).astype(np.float32).astype(dtype).astype(np.float64)
    return np.moveaxis((codes * scale).reshape(v.shape), -1, axis)


WIDE = False


def mx_kscale(k):
    if not WIDE:
        return np.ones(k)
    levels = np.array([10, -10, 5, -5, 0])
    if k % 512:
        return np.exp2(np.random.permutation(np.resize(levels, k // 32))).repeat(32)
    a = np.empty((k // 512, 16))
    for p in range(k // 512):
        a[p, :8] = np.random.permutation(np.resize(levels, 8))
        for g in range(8):
            far = levels[np.abs(levels - a[p, g]) >= 10]
            a[p, g + 8] = far[np.random.randint(len(far))]
    return np.exp2(a.ravel()).repeat(32)


def f64(x):
    return np.asarray(x).astype(np.float64)


def striped(idx):
    return np.tile(idx.reshape(-1, 16).T, (8, 1)).astype(np.uint16)


def unstriped(offs):
    return offs[:16].T.reshape(-1).astype(np.int64)


def silu(v):
    return v / (1.0 + np.exp(-np.maximum(v, -700.0)))


K, T, D, S, V, N = 512, 4096, 4, 3584, 896, 512


def setup_inputs():
    n = np.random.standard_normal
    s = mx_kscale(K)[:, None]
    return {
        "xT": (n((K, T)) * s).astype(np.float32),
        "w": (n((D, K, N)) / np.sqrt(D * K) / s[None]).astype(np.float32),
        "b": (0.3 * n((N, 1))).astype(np.float32),
        "offs": striped(np.random.permutation(T)[:S]),
    }


def reference(xT, w, b, offs):
    idx = unstriped(offs)
    xq = mxq(f64(xT)[:, idx], 0, "e4m3")
    wq = mxq(f64(w), 1, "e4m3")
    y = sum(wq[d].T @ xq[:, d * V:(d + 1) * V] for d in range(D))
    y = silu(y + f64(b))
    return y

@@ -1,0 +1,158 @@
+from contextlib import ExitStack
+
+import concourse.mybir as mybir
+
+K, T, D, S, V, N = 512, 4096, 4, 3584, 896, 512
+FLOPS = 2 * K * S * N
+
+F32 = mybir.dt.float32
+BF16 = mybir.dt.bfloat16
+U32 = mybir.dt.uint32
+U16 = mybir.dt.uint16
+U8 = mybir.dt.uint8
+FP8X4 = mybir.dt.float8_e4m3fn_x4
+ACT = mybir.ActivationFunctionType
+
+P = 128
+PACK = 4
+RUN = 4
+LIST_ROWS = 16
+
+X_CHUNKS = [(1024, 384), (1024, 384), (1024, 384), (512, 192), (256, 96), (256, 96)]
+GATHER_EDGES = [0, 1152, 2176, 3072, 3584]
+AFTER = {1: 0, 2: 2, 3: 3}
+EARLY = 384
+
+
+def interleave_views(grouped, raw, lo, hi):
+    dst = grouped[:, lo:hi, :].rearrange("p (c i) t -> p c t i", i=RUN)
+    src = raw[:, :, lo:hi].rearrange("p t (c i) -> p c t i", i=RUN)
+    return dst, src
+
+
+def tile_picked_merge_lin_silu_sub_e_kernel(tc, xT, w, b, offs, out):
+    nc = tc.nc
+    with ExitStack() as ctx:
+        keep = ctx.enter_context(tc.tile_pool(name="keep", bufs=1))
+        psum = ctx.enter_context(tc.psum_pool(name="psum", bufs=1))
+
+        offsets = keep.tile([P, S // LIST_ROWS], U16, name="offsets")
+        x_codes = keep.tile([P, T], U32, name="x_codes", align_bytes=64)
+        x_scales = keep.tile([P, T], U8, name="x_scales", align_bytes=64)
+        bias = keep.tile([P, N // P], F32, name="bias")
+
+        warm_in = keep.tile([P, 8], F32, name="warm_in")
+        warm_out = keep.tile([P, 8], F32, name="warm_out")
+        nc.vector.memset(warm_in[:], 0.0)
+        nc.scalar.activation(warm_out[:], warm_in[:], ACT.Silu)
+
+        nc.gpsimd.memset(x_scales[:], 0)
+
+        x_rows = xT.rearrange("(p t) c -> p t c", t=PACK)
+        x_raw = []
+        first = 0
+        for i, (width, share) in enumerate(X_CHUNKS):
+            raw = keep.tile([P, PACK, width], F32, name="x_raw%d" % i)
+            nc.sync.dma_start(out=raw[:], in_=x_rows[:, :, first : first + width])
+            x_raw.append(raw)
+            first += width
+        nc.sync.dma_start(offsets[:], offs)
+        w_raw = []
+        for d in range(D):
+            raw = keep.tile([P, PACK, N], F32, name="w_raw%d" % d, tag="w_raw%d" % d, align_bytes=64)
+            nc.sync.dma_start(out=raw[:], in_=w[d].rearrange("(p t) m -> p t m", t=PACK))
+            w_raw.append(raw)
+        with nc.allow_non_contiguous_dma(reason="one bias value a partition and block"):
+            nc.sync.dma_start(out=bias[:], in_=b.rearrange("(c p) o -> p (c o)", p=P))
+
+        first = 0
+        for i, (width, share) in enumerate(X_CHUNKS):
+            grouped = keep.tile([P, width, PACK], BF16, name="x_bf%d" % i, align_bytes=64)
+            dst, src = interleave_views(grouped, x_raw[i], 0, share)
+            nc.scalar.activation(dst, src, ACT.Copy)
+            dst, src = interleave_views(grouped, x_raw[i], share, width)
+            nc.vector.tensor_copy(dst, src)
+            cols = slice(first, first + width)
+            nc.vector.quantize_mx(
+                out=x_codes[:, cols].bitcast(FP8X4),
+                scales=x_scales[:, cols],
+                in_=grouped[:].rearrange("p c t -> p (c t)"),
+            )
+            first += width
+
+        w_codes = [keep.tile([P, N], U32, name="w_codes%d" % d, align_bytes=64) for d in range(D)]
+        w_scales = [keep.tile([P, N], U8, name="w_scales%d" % d, align_bytes=64) for d in range(D)]
+        early = [psum.tile([P, 512], F32, name="early%d" % c) for c in range(N // P)]
+        late = [psum.tile([P, 512], F32, name="late%d" % c) for c in range(N // P)]
+
+        def quantize_w(d):
+            grouped = keep.tile([P, N, PACK], BF16, name="w_bf%d" % d, tag="w_bf%d" % d, align_bytes=64)
+            dst, src = interleave_views(grouped, w_raw[d], 0, N)
+            nc.scalar.activation(dst, src, ACT.Copy)
+            nc.vector.quantize_mx(
+                out=w_codes[d][:].bitcast(FP8X4),
+                scales=w_scales[d][:],
+                in_=grouped[:].rearrange("p c t -> p (c t)"),
+            )
+
+        picked = []
+
+        def gather(g):
+            lo, hi = GATHER_EDGES[g], GATHER_EDGES[g + 1]
+            entries = offsets[:, lo // LIST_ROWS : hi // LIST_ROWS]
+            scale_tag = "w_raw%d" % AFTER[g] if g in AFTER else "picked_scales"
+            code_tag = "w_bf%d" % AFTER[g] if g in AFTER else "picked_codes"
+            scales = keep.tile([P, hi - lo], U8, name="picked_scales%d" % g, tag=scale_tag, align_bytes=64)
+            codes = keep.tile([P, hi - lo], U32, name="picked_codes%d" % g, tag=code_tag, align_bytes=64)
+            nc.vector.tensor_copy(scales[:], x_scales[:].indirect(entries))
+            nc.vector.tensor_copy(codes[:], x_codes[:].indirect(entries))
+            picked.append((lo, hi, codes, scales))
+
+        def product(acc, d, c, lo, hi, start, stop):
+            rows = slice(c * P, (c + 1) * P)
+            base, end, codes, scales = [g for g in picked if g[0] <= d * V + lo < g[1]][0]
+            assert d * V + hi <= end
+            cols = slice(d * V + lo - base, d * V + hi - base)
+            nc.tensor.matmul_mx(
+                out=acc,
+                lhsT=w_codes[d][:, rows].bitcast(FP8X4),
+                lhsT_scale=w_scales[d][:, rows],
+                rhs=codes[:, cols].bitcast(FP8X4),
+                rhs_scale=scales[:, cols],
+                start=start,
+                stop=stop,
+            )
+
+        def early_products(d):
+            for c in range(N // P):
+                product(early[c][:, 0:256], d, c, 0, 256, d == 0, False)
+                product(early[c][:, 256:EARLY], d, c, 256, EARLY, False, d == D - 1)
+
+        def late_products(d):
+            for c in range(N // P):
+                product(late[c][:], d, c, EARLY, V, d == 0, d == D - 1)
+
+        def finish(acc, lo, hi, tag):
+            for c in range(N // P):
+                y = keep.tile([P, hi - lo], F32, name="y_%s%d" % (tag, c))
+                nc.scalar.activation(y[:], acc[c][:, 0 : hi - lo], ACT.Silu, bias=bias[:, c : c + 1])
+                nc.sync.dma_start(out=out[c * P : (c + 1) * P, lo:hi], in_=y[:])
+
+        gather(0)
+        quantize_w(0)
+        early_products(0)
+        late_products(0)
+        gather(1)
+        quantize_w(1)
+        early_products(1)
+        late_products(1)
+        quantize_w(2)
+        early_products(2)
+        gather(2)
+        quantize_w(3)
+        early_products(3)
+        finish(early, 0, EARLY, "early")
+        late_products(2)
+        gather(3)
+        late_products(3)
+        finish(late, EARLY, V, "late")

@@ -17,17 +17,13 @@ P = 128
 PACK = 4
 RUN = 4
 LIST_ROWS = 16
+BLOCKS = N // P
+WARM = 4
 
-X_CHUNKS = [(1024, 384), (1024, 384), (1024, 384), (512, 192), (256, 96), (256, 96)]
-GATHER_EDGES = [0, 1152, 2176, 3072, 3584]
-AFTER = {1: 0, 2: 2, 3: 3}
-EARLY = 384
-
-
-def interleave_views(grouped, raw, lo, hi):
-    dst = grouped[:, lo:hi, :].rearrange("p (c i) t -> p c t i", i=RUN)
-    src = raw[:, :, lo:hi].rearrange("p t (c i) -> p c t i", i=RUN)
-    return dst, src
+X_CHUNKS = [
+    [(2048, 704), (1536, 512), (512, 160)],
+    [(1024, 1024), (1024, 1024), (1024, 1024), (512, 384), (512, 0)],
+]
 
 
 def tile_picked_merge_lin_silu_sub_e_kernel(tc, xT, w, b, offs, out):
@@ -37,122 +33,152 @@ def tile_picked_merge_lin_silu_sub_e_kernel(tc, xT, w, b, offs, out):
         psum = ctx.enter_context(tc.psum_pool(name="psum", bufs=1))
 
         offsets = keep.tile([P, S // LIST_ROWS], U16, name="offsets")
-        x_codes = keep.tile([P, T], U32, name="x_codes", align_bytes=64)
-        x_scales = keep.tile([P, T], U8, name="x_scales", align_bytes=64)
-        bias = keep.tile([P, N // P], F32, name="bias")
+        bias = keep.tile([P, BLOCKS], F32, name="bias")
 
         warm_in = keep.tile([P, 8], F32, name="warm_in")
         warm_out = keep.tile([P, 8], F32, name="warm_out")
         nc.vector.memset(warm_in[:], 0.0)
         nc.scalar.activation(warm_out[:], warm_in[:], ACT.Silu)
 
-        nc.gpsimd.memset(x_scales[:], 0)
-
         x_rows = xT.rearrange("(p t) c -> p t c", t=PACK)
-        x_raw = []
-        first = 0
-        for i, (width, share) in enumerate(X_CHUNKS):
-            raw = keep.tile([P, PACK, width], F32, name="x_raw%d" % i)
-            nc.sync.dma_start(out=raw[:], in_=x_rows[:, :, first : first + width])
-            x_raw.append(raw)
-            first += width
-        nc.sync.dma_start(offsets[:], offs)
+        x_raw = [[], []]
+        for u in range(2):
+            first = 0
+            for i, (width, share) in enumerate(X_CHUNKS[u]):
+                raw = keep.tile([P, 2, width], F32, name="x_raw%d_%d" % (u, i))
+                nc.sync.dma_start(out=raw[:], in_=x_rows[:, 2 * u : 2 * u + 2, first : first + width])
+                x_raw[u].append(raw)
+                first += width
+            if u == 0:
+                nc.sync.dma_start(offsets[:], offs)
         w_raw = []
         for d in range(D):
-            raw = keep.tile([P, PACK, N], F32, name="w_raw%d" % d, tag="w_raw%d" % d, align_bytes=64)
+            raw = keep.tile([P, PACK, N], F32, name="w_raw%d" % d)
             nc.sync.dma_start(out=raw[:], in_=w[d].rearrange("(p t) m -> p t m", t=PACK))
             w_raw.append(raw)
         with nc.allow_non_contiguous_dma(reason="one bias value a partition and block"):
             nc.sync.dma_start(out=bias[:], in_=b.rearrange("(c p) o -> p (c o)", p=P))
 
-        first = 0
-        for i, (width, share) in enumerate(X_CHUNKS):
-            grouped = keep.tile([P, width, PACK], BF16, name="x_bf%d" % i, align_bytes=64)
-            dst, src = interleave_views(grouped, x_raw[i], 0, share)
-            nc.scalar.activation(dst, src, ACT.Copy)
-            dst, src = interleave_views(grouped, x_raw[i], share, width)
-            nc.vector.tensor_copy(dst, src)
-            cols = slice(first, first + width)
-            nc.vector.quantize_mx(
-                out=x_codes[:, cols].bitcast(FP8X4),
-                scales=x_scales[:, cols],
-                in_=grouped[:].rearrange("p c t -> p (c t)"),
-            )
-            first += width
+        pairs = [keep.tile([P, T, 2], BF16, name="pairs%d" % u, align_bytes=64) for u in range(2)]
+        picked = [keep.tile([P, 2, N * PACK], BF16, name="picked%d" % d, align_bytes=64) for d in range(D)]
 
-        w_codes = [keep.tile([P, N], U32, name="w_codes%d" % d, align_bytes=64) for d in range(D)]
-        w_scales = [keep.tile([P, N], U8, name="w_scales%d" % d, align_bytes=64) for d in range(D)]
-        early = [psum.tile([P, 512], F32, name="early%d" % c) for c in range(N // P)]
-        late = [psum.tile([P, 512], F32, name="late%d" % c) for c in range(N // P)]
+        def round_pair(u):
+            first = 0
+            for i, (width, share) in enumerate(X_CHUNKS[u]):
+                src = x_raw[u][i][:].rearrange("p e c -> p c e")
+                if share > 0:
+                    nc.scalar.activation(pairs[u][:, first : first + share, :], src[:, 0:share, :], ACT.Copy)
+                if share < width:
+                    nc.vector.tensor_copy(pairs[u][:, first + share : first + width, :], src[:, share:width, :])
+                first += width
 
-        def quantize_w(d):
-            grouped = keep.tile([P, N, PACK], BF16, name="w_bf%d" % d, tag="w_bf%d" % d, align_bytes=64)
-            dst, src = interleave_views(grouped, w_raw[d], 0, N)
-            nc.scalar.activation(dst, src, ACT.Copy)
-            nc.vector.quantize_mx(
-                out=w_codes[d][:].bitcast(FP8X4),
-                scales=w_scales[d][:],
-                in_=grouped[:].rearrange("p c t -> p (c t)"),
+        def gather(u, d):
+            window = pairs[u][:].rearrange("p c e -> p (c e)").bitcast(U32)
+            entries = offsets[:, d * V // LIST_ROWS : (d + 1) * V // LIST_ROWS]
+            nc.vector.tensor_copy(picked[d][:, u, 0 : 2 * V].bitcast(U32), window.indirect(entries))
+
+        def interleave(copy, dst, d, lo, hi):
+            copy(
+                dst.rearrange("p c (u e) -> p c u e", e=2),
+                picked[d][:, :, 2 * lo : 2 * hi].rearrange("p u (c e) -> p c u e", e=2),
             )
 
-        picked = []
+        def quantize(name, grouped, width, codes_tag=""):
+            codes = keep.tile([P, width], U32, name=name + "_codes", tag=codes_tag, align_bytes=64)
+            scales = keep.tile([P, width], U8, name=name + "_scales", align_bytes=64)
+            nc.vector.quantize_mx(out=codes[:].bitcast(FP8X4), scales=scales[:], in_=grouped)
+            return codes, scales
 
-        def gather(g):
-            lo, hi = GATHER_EDGES[g], GATHER_EDGES[g + 1]
-            entries = offsets[:, lo // LIST_ROWS : hi // LIST_ROWS]
-            scale_tag = "w_raw%d" % AFTER[g] if g in AFTER else "picked_scales"
-            code_tag = "w_bf%d" % AFTER[g] if g in AFTER else "picked_codes"
-            scales = keep.tile([P, hi - lo], U8, name="picked_scales%d" % g, tag=scale_tag, align_bytes=64)
-            codes = keep.tile([P, hi - lo], U32, name="picked_codes%d" % g, tag=code_tag, align_bytes=64)
-            nc.vector.tensor_copy(scales[:], x_scales[:].indirect(entries))
-            nc.vector.tensor_copy(codes[:], x_codes[:].indirect(entries))
-            picked.append((lo, hi, codes, scales))
+        w_mx = {}
 
-        def product(acc, d, c, lo, hi, start, stop):
+        def quantize_w(d, grouped):
+            nc.scalar.activation(
+                grouped.rearrange("p (c i t) -> p c t i", i=RUN, t=PACK),
+                w_raw[d][:].rearrange("p t (c i) -> p c t i", i=RUN),
+                ACT.Copy,
+            )
+            w_mx[d] = quantize("w%d" % d, grouped, N, "wide_bf%d" % (d - 1) if d else "")
+
+        def product(acc, d, c, x_mx, cols, start, stop):
             rows = slice(c * P, (c + 1) * P)
-            base, end, codes, scales = [g for g in picked if g[0] <= d * V + lo < g[1]][0]
-            assert d * V + hi <= end
-            cols = slice(d * V + lo - base, d * V + hi - base)
             nc.tensor.matmul_mx(
                 out=acc,
-                lhsT=w_codes[d][:, rows].bitcast(FP8X4),
-                lhsT_scale=w_scales[d][:, rows],
-                rhs=codes[:, cols].bitcast(FP8X4),
-                rhs_scale=scales[:, cols],
+                lhsT=w_mx[d][0][:, rows].bitcast(FP8X4),
+                lhsT_scale=w_mx[d][1][:, rows],
+                rhs=x_mx[0][:, cols].bitcast(FP8X4),
+                rhs_scale=x_mx[1][:, cols],
                 start=start,
                 stop=stop,
             )
 
-        def early_products(d):
-            for c in range(N // P):
-                product(early[c][:, 0:256], d, c, 0, 256, d == 0, False)
-                product(early[c][:, 256:EARLY], d, c, 256, EARLY, False, d == D - 1)
+        def tokens(name, pieces, grouped, copy=nc.vector.tensor_copy):
+            first = 0
+            for d, lo, hi in pieces:
+                dst = grouped[:, first * PACK : (first + hi - lo) * PACK]
+                interleave(copy, dst.rearrange("p (c t) -> p c t", t=PACK), d, lo, hi)
+                first += hi - lo
+            return quantize(name, grouped, first)
 
-        def late_products(d):
-            for c in range(N // P):
-                product(late[c][:], d, c, EARLY, V, d == 0, d == D - 1)
+        out_blocks = out.rearrange("(c p) v -> p c v", p=P)
+        wide = [psum.tile([P, 512], F32, name="wide%d" % c) for c in range(BLOCKS)]
+        mid = [psum.tile([P, 2, 256], F32, name="mid%d" % j) for j in range(2)]
+        last = [psum.tile([P, 2, 128], F32, name="last%d" % j) for j in range(2)]
 
-        def finish(acc, lo, hi, tag):
-            for c in range(N // P):
-                y = keep.tile([P, hi - lo], F32, name="y_%s%d" % (tag, c))
-                nc.scalar.activation(y[:], acc[c][:, 0 : hi - lo], ACT.Silu, bias=bias[:, c : c + 1])
-                nc.sync.dma_start(out=out[c * P : (c + 1) * P, lo:hi], in_=y[:])
+        round_pair(0)
+        for d in range(D):
+            gather(0, d)
+        round_pair(1)
 
-        gather(0)
-        quantize_w(0)
-        early_products(0)
-        late_products(0)
-        gather(1)
-        quantize_w(1)
-        early_products(1)
-        late_products(1)
-        quantize_w(2)
-        early_products(2)
-        gather(2)
-        quantize_w(3)
-        early_products(3)
-        finish(early, 0, EARLY, "early")
-        late_products(2)
-        gather(3)
-        late_products(3)
-        finish(late, EARLY, V, "late")
+        w_own = [keep.tile([P, N * PACK], BF16, name="w_bf%d" % d, align_bytes=64) for d in (1, 3)]
+        w_grouped = [picked[2][:, 1, :], w_own[0][:], picked[3][:, 1, :], w_own[1][:]]
+
+        WIDE_COPY = [nc.vector.tensor_copy, nc.vector.tensor_copy, nc.vector.tensor_copy]
+        halves = [keep.tile([P, 256 * PACK], BF16, name="half_bf%d" % h, align_bytes=64) for h in range(2)]
+        gather(1, 0)
+        gather(1, 1)
+        for d in range(D - 1):
+            quantize_w(d, w_grouped[d])
+            grouped = keep.tile([P, 512 * PACK], BF16, name="wide_bf%d" % d, tag="wide_bf%d" % d, align_bytes=64)
+            x_mx = tokens("wide_x%d" % d, [(d, 0, 512)], grouped[:], WIDE_COPY[d])
+            for c in range(BLOCKS):
+                product(wide[c][:], d, c, x_mx, slice(0, 512), d == 0, False)
+            if d == 0:
+                gather(1, 2)
+        for c in range(WARM):
+            product(last[c % 2][:].rearrange("p i v -> p (i v)"), 2, c, x_mx, slice(0, 256), True, True)
+            product(mid[c % 2][:, 0, :], 2, c, x_mx, slice(256, 512), True, True)
+        gather(1, 3)
+        quantize_w(3, w_grouped[3])
+        for h in range(2):
+            x_mx = tokens("wide_x3_%d" % h, [(3, 256 * h, 256 * h + 256)], halves[h][:])
+            for c in range(BLOCKS):
+                product(wide[c][:, 256 * h : 256 * h + 256], 3, c, x_mx, slice(0, 256), False, h == 1)
+        for c in range(BLOCKS):
+            y = keep.tile([P, 512], F32, name="y_wide%d" % c)
+            nc.scalar.activation(y[:], wide[c][:], ACT.Silu, bias=bias[:, c : c + 1])
+            nc.sync.dma_start(out=out_blocks[:, c, 0:512], in_=y[:])
+
+        chain = [halves[0][:], halves[1][:]]
+        for d in range(D):
+            x_mx = tokens("mid_x%d" % d, [(d, 512, 768)], chain[d % 2])
+            for c in range(BLOCKS):
+                product(mid[c // 2][:, c % 2, :], d, c, x_mx, slice(0, 256), d == 0 and c % 2 == 0, d == D - 1 and c % 2 == 1)
+        for j in range(2):
+            y = keep.tile([P, 2, 256], F32, name="y_mid%d" % j)
+            for i in range(2):
+                c = 2 * j + i
+                nc.scalar.activation(y[:, i, :], mid[j][:, i, :], ACT.Silu, bias=bias[:, c : c + 1])
+            nc.sync.dma_start(out=out_blocks[:, 2 * j : 2 * j + 2, 512:768], in_=y[:])
+
+        for h in range(2):
+            x_mx = tokens("last_x%d" % h, [(2 * h, 768, V), (2 * h + 1, 768, V)], chain[h])
+            for c in range(BLOCKS):
+                for i in range(2):
+                    d = 2 * h + i
+                    product(last[c // 2][:, c % 2, :], d, c, x_mx, slice(128 * i, 128 * i + 128), d == 0 and c % 2 == 0, d == D - 1 and c % 2 == 1)
+        for j in range(2):
+            y = keep.tile([P, 2, 128], F32, name="y_last%d" % j)
+            for i in range(2):
+                c = 2 * j + i
+                nc.scalar.activation(y[:, i, :], last[j][:, i, :], ACT.Silu, bias=bias[:, c : c + 1])
+            nc.sync.dma_start(out=out_blocks[:, 2 * j : 2 * j + 2, 768:V], in_=y[:])

@@ -65,11 +65,13 @@ def tile_picked_merge_lin_silu_sub_e_kernel(tc, xT, w, b, offs, out):
         def round_pair(u):
             first = 0
             for i, (width, share) in enumerate(X_CHUNKS[u]):
-                src = x_raw[u][i][:].rearrange("p e c -> p c e")
+                src = x_raw[u][i][:].rearrange("p e (c i) -> p c e i", i=RUN)
+                dst = pairs[u][:, first : first + width, :].rearrange("p (c i) e -> p c e i", i=RUN)
+                cut = share // RUN
                 if share > 0:
-                    nc.scalar.activation(pairs[u][:, first : first + share, :], src[:, 0:share, :], ACT.Copy)
+                    nc.scalar.activation(dst[:, :cut], src[:, :cut], ACT.Copy)
                 if share < width:
-                    nc.vector.tensor_copy(pairs[u][:, first + share : first + width, :], src[:, share:width, :])
+                    nc.vector.tensor_copy(dst[:, cut:], src[:, cut:])
                 first += width
 
         def gather(u, d):
@@ -79,8 +81,8 @@ def tile_picked_merge_lin_silu_sub_e_kernel(tc, xT, w, b, offs, out):
 
         def interleave(copy, dst, d, lo, hi):
             copy(
-                dst.rearrange("p c (u e) -> p c u e", e=2),
-                picked[d][:, :, 2 * lo : 2 * hi].rearrange("p u (c e) -> p c u e", e=2),
+                dst.rearrange("p (c i) (u e) -> p c u i e", i=2, e=2),
+                picked[d][:, :, 2 * lo : 2 * hi].rearrange("p u (c i e) -> p c u i e", i=2, e=2),
             )
 
         def quantize(name, grouped, width, codes_tag=""):
@@ -91,20 +93,24 @@ def tile_picked_merge_lin_silu_sub_e_kernel(tc, xT, w, b, offs, out):
 
         w_mx = {}
 
-        def quantize_w(d, grouped):
+        def round_w(d, grouped):
             nc.scalar.activation(
                 grouped.rearrange("p (c i t) -> p c t i", i=RUN, t=PACK),
                 w_raw[d][:].rearrange("p t (c i) -> p c t i", i=RUN),
                 ACT.Copy,
             )
-            w_mx[d] = quantize("w%d" % d, grouped, N, "wide_bf%d" % (d - 1) if d else "")
+
+        def quantize_w(d, grouped):
+            round_w(d, grouped)
+            codes, scales = quantize("w%d" % d, grouped, N, "wide_bf%d" % (d - 1) if d else "")
+            for c in range(BLOCKS):
+                w_mx[d, c] = (codes[:, c * P : (c + 1) * P], scales[:, c * P : (c + 1) * P])
 
         def product(acc, d, c, x_mx, cols, start, stop):
-            rows = slice(c * P, (c + 1) * P)
             nc.tensor.matmul_mx(
                 out=acc,
-                lhsT=w_mx[d][0][:, rows].bitcast(FP8X4),
-                lhsT_scale=w_mx[d][1][:, rows],
+                lhsT=w_mx[d, c][0].bitcast(FP8X4),
+                lhsT_scale=w_mx[d, c][1],
                 rhs=x_mx[0][:, cols].bitcast(FP8X4),
                 rhs_scale=x_mx[1][:, cols],
                 start=start,
@@ -133,7 +139,7 @@ def tile_picked_merge_lin_silu_sub_e_kernel(tc, xT, w, b, offs, out):
         w_grouped = [picked[2][:, 1, :], w_own[0][:], picked[3][:, 1, :], w_own[1][:]]
 
         WIDE_COPY = [nc.vector.tensor_copy, nc.vector.tensor_copy, nc.vector.tensor_copy]
-        halves = [keep.tile([P, 256 * PACK], BF16, name="half_bf%d" % h, align_bytes=64) for h in range(2)]
+        halves = [keep.tile([P, 256 * PACK], BF16, name="half_bf%d" % h, tag="half_bf%d" % h, align_bytes=64) for h in range(2)]
         gather(1, 0)
         gather(1, 1)
         for d in range(D - 1):
@@ -148,17 +154,29 @@ def tile_picked_merge_lin_silu_sub_e_kernel(tc, xT, w, b, offs, out):
             product(last[c % 2][:].rearrange("p i v -> p (i v)"), 2, c, x_mx, slice(0, 256), True, True)
             product(mid[c % 2][:, 0, :], 2, c, x_mx, slice(256, 512), True, True)
         gather(1, 3)
-        quantize_w(3, w_grouped[3])
-        for h in range(2):
-            x_mx = tokens("wide_x3_%d" % h, [(3, 256 * h, 256 * h + 256)], halves[h][:])
-            for c in range(BLOCKS):
-                product(wide[c][:, 256 * h : 256 * h + 256], 3, c, x_mx, slice(0, 256), False, h == 1)
+        round_w(3, w_grouped[3])
+        codes, scales = quantize("w3_first", w_grouped[3][:, 0 : P * PACK], P, "wide_bf2")
+        w_mx[3, 0] = (codes[:], scales[:])
+        x_halves = [tokens("wide_x3_%d" % h, [(3, 256 * h, 256 * h + 256)], halves[h][:]) for h in range(2)]
+        codes = keep.tile([P, N - P], U32, name="w3_rest_codes", tag="half_bf0", align_bytes=64)
+        scales = keep.tile([P, N - P], U8, name="w3_rest_scales", align_bytes=64)
+        for lo, hi in ((P, 2 * P), (2 * P, N)):
+            nc.vector.quantize_mx(
+                out=codes[:, lo - P : hi - P].bitcast(FP8X4),
+                scales=scales[:, lo - P : hi - P],
+                in_=w_grouped[3][:, lo * PACK : hi * PACK],
+            )
+        for c in range(1, BLOCKS):
+            w_mx[3, c] = (codes[:, (c - 1) * P : c * P], scales[:, (c - 1) * P : c * P])
+        for c in range(BLOCKS):
+            for h in range(2):
+                product(wide[c][:, 256 * h : 256 * h + 256], 3, c, x_halves[h], slice(0, 256), False, h == 1)
         for c in range(BLOCKS):
             y = keep.tile([P, 512], F32, name="y_wide%d" % c)
             nc.scalar.activation(y[:], wide[c][:], ACT.Silu, bias=bias[:, c : c + 1])
             nc.sync.dma_start(out=out_blocks[:, c, 0:512], in_=y[:])
 
-        chain = [halves[0][:], halves[1][:]]
+        chain = [halves[1][:], w_own[1][:, 256 * PACK :]]
         for d in range(D):
             x_mx = tokens("mid_x%d" % d, [(d, 512, 768)], chain[d % 2])
             for c in range(BLOCKS):

@@ -53,7 +53,7 @@ def tile_picked_merge_lin_silu_sub_e_kernel(tc, xT, w, b, offs, out):
                 nc.sync.dma_start(offsets[:], offs)
         w_raw = []
         for d in range(D):
-            raw = keep.tile([P, PACK, N], F32, name="w_raw%d" % d)
+            raw = keep.tile([P, PACK, N], F32, name="w_raw%d" % d, tag="w_raw%d" % d, align_bytes=64)
             nc.sync.dma_start(out=raw[:], in_=w[d].rearrange("(p t) m -> p t m", t=PACK))
             w_raw.append(raw)
         with nc.allow_non_contiguous_dma(reason="one bias value a partition and block"):
@@ -102,7 +102,7 @@ def tile_picked_merge_lin_silu_sub_e_kernel(tc, xT, w, b, offs, out):
 
         def quantize_w(d, grouped):
             round_w(d, grouped)
-            codes, scales = quantize("w%d" % d, grouped, N, "wide_bf%d" % (d - 1) if d else "")
+            codes, scales = quantize("w%d" % d, grouped, N)
             for c in range(BLOCKS):
                 w_mx[d, c] = (codes[:, c * P : (c + 1) * P], scales[:, c * P : (c + 1) * P])
 
@@ -117,13 +117,13 @@ def tile_picked_merge_lin_silu_sub_e_kernel(tc, xT, w, b, offs, out):
                 stop=stop,
             )
 
-        def tokens(name, pieces, grouped, copy=nc.vector.tensor_copy):
+        def tokens(name, pieces, grouped, copy=nc.vector.tensor_copy, codes_tag=""):
             first = 0
             for d, lo, hi in pieces:
                 dst = grouped[:, first * PACK : (first + hi - lo) * PACK]
                 interleave(copy, dst.rearrange("p (c t) -> p c t", t=PACK), d, lo, hi)
                 first += hi - lo
-            return quantize(name, grouped, first)
+            return quantize(name, grouped, first, codes_tag)
 
         out_blocks = out.rearrange("(c p) v -> p c v", p=P)
         wide = [psum.tile([P, 512], F32, name="wide%d" % c) for c in range(BLOCKS)]
@@ -139,13 +139,12 @@ def tile_picked_merge_lin_silu_sub_e_kernel(tc, xT, w, b, offs, out):
         w_grouped = [picked[2][:, 1, :], w_own[0][:], picked[3][:, 1, :], w_own[1][:]]
 
         WIDE_COPY = [nc.vector.tensor_copy, nc.vector.tensor_copy, nc.vector.tensor_copy]
-        halves = [keep.tile([P, 256 * PACK], BF16, name="half_bf%d" % h, tag="half_bf%d" % h, align_bytes=64) for h in range(2)]
         gather(1, 0)
         gather(1, 1)
         for d in range(D - 1):
             quantize_w(d, w_grouped[d])
             grouped = keep.tile([P, 512 * PACK], BF16, name="wide_bf%d" % d, tag="wide_bf%d" % d, align_bytes=64)
-            x_mx = tokens("wide_x%d" % d, [(d, 0, 512)], grouped[:], WIDE_COPY[d])
+            x_mx = tokens("wide_x%d" % d, [(d, 0, 512)], grouped[:], WIDE_COPY[d], ["w_raw0", "wide_bf0", "w_raw2"][d])
             for c in range(BLOCKS):
                 product(wide[c][:], d, c, x_mx, slice(0, 512), d == 0, False)
             if d == 0:
@@ -155,19 +154,15 @@ def tile_picked_merge_lin_silu_sub_e_kernel(tc, xT, w, b, offs, out):
             product(mid[c % 2][:, 0, :], 2, c, x_mx, slice(256, 512), True, True)
         gather(1, 3)
         round_w(3, w_grouped[3])
-        codes, scales = quantize("w3_first", w_grouped[3][:, 0 : P * PACK], P, "wide_bf2")
-        w_mx[3, 0] = (codes[:], scales[:])
-        x_halves = [tokens("wide_x3_%d" % h, [(3, 256 * h, 256 * h + 256)], halves[h][:]) for h in range(2)]
-        codes = keep.tile([P, N - P], U32, name="w3_rest_codes", tag="half_bf0", align_bytes=64)
-        scales = keep.tile([P, N - P], U8, name="w3_rest_scales", align_bytes=64)
-        for lo, hi in ((P, 2 * P), (2 * P, N)):
-            nc.vector.quantize_mx(
-                out=codes[:, lo - P : hi - P].bitcast(FP8X4),
-                scales=scales[:, lo - P : hi - P],
-                in_=w_grouped[3][:, lo * PACK : hi * PACK],
-            )
-        for c in range(1, BLOCKS):
-            w_mx[3, c] = (codes[:, (c - 1) * P : c * P], scales[:, (c - 1) * P : c * P])
+        chain = [w_grouped[3][:, 0 : 256 * PACK], w_grouped[3][:, 256 * PACK :]]
+        front = quantize("w3_front", chain[0], 256)
+        half = keep.tile([P, 256 * PACK], BF16, name="half_bf", tag="w_raw3", align_bytes=64)
+        x_halves = [tokens("wide_x3_0", [(3, 0, 256)], half[:]), tokens("wide_x3_1", [(3, 256, 512)], chain[0])]
+        back = quantize("w3_back", chain[1], 256, "w_raw3")
+        for c in range(BLOCKS):
+            codes, scales = (front, back)[c // 2]
+            cols = slice(c % 2 * P, (c % 2 + 1) * P)
+            w_mx[3, c] = (codes[:, cols], scales[:, cols])
         for c in range(BLOCKS):
             for h in range(2):
                 product(wide[c][:, 256 * h : 256 * h + 256], 3, c, x_halves[h], slice(0, 256), False, h == 1)
@@ -176,7 +171,6 @@ def tile_picked_merge_lin_silu_sub_e_kernel(tc, xT, w, b, offs, out):
             nc.scalar.activation(y[:], wide[c][:], ACT.Silu, bias=bias[:, c : c + 1])
             nc.sync.dma_start(out=out_blocks[:, c, 0:512], in_=y[:])
 
-        chain = [halves[1][:], w_own[1][:, 256 * PACK :]]
         for d in range(D):
             x_mx = tokens("mid_x%d" % d, [(d, 512, 768)], chain[d % 2])
             for c in range(BLOCKS):

@@ -22,7 +22,7 @@ WARM = 4
 
 X_CHUNKS = [
     [(2048, 704), (1536, 512), (512, 160)],
-    [(1024, 1024), (1024, 1024), (1024, 1024), (512, 384), (512, 0)],
+    [(1024, 1024), (1024, 1024), (1024, 1024), (768, 256), (256, 0)],
 ]
 
 
@@ -52,9 +52,13 @@ def tile_picked_merge_lin_silu_sub_e_kernel(tc, xT, w, b, offs, out):
             if u == 0:
                 nc.sync.dma_start(offsets[:], offs)
         w_raw = []
-        for d in range(D):
+        for d in range(D - 1):
             raw = keep.tile([P, PACK, N], F32, name="w_raw%d" % d, tag="w_raw%d" % d, align_bytes=64)
             nc.sync.dma_start(out=raw[:], in_=w[d].rearrange("(p t) m -> p t m", t=PACK))
+            w_raw.append(raw)
+        for h in range(2):
+            raw = keep.tile([P, PACK, 256], F32, name="w_raw3_%d" % h, tag="w_raw3_%d" % h, align_bytes=64)
+            nc.sync.dma_start(out=raw[:], in_=w[3].rearrange("(p t) m -> p t m", t=PACK)[:, :, 256 * h : 256 * h + 256])
             w_raw.append(raw)
         with nc.allow_non_contiguous_dma(reason="one bias value a partition and block"):
             nc.sync.dma_start(out=bias[:], in_=b.rearrange("(c p) o -> p (c o)", p=P))
@@ -127,38 +131,41 @@ def tile_picked_merge_lin_silu_sub_e_kernel(tc, xT, w, b, offs, out):
 
         out_blocks = out.rearrange("(c p) v -> p c v", p=P)
         wide = [psum.tile([P, 512], F32, name="wide%d" % c) for c in range(BLOCKS)]
-        mid = [psum.tile([P, 2, 256], F32, name="mid%d" % j) for j in range(2)]
-        last = [psum.tile([P, 2, 128], F32, name="last%d" % j) for j in range(2)]
+        mid = [psum.tile([P, 512], F32, name="mid%d" % c) for c in range(BLOCKS)]
 
         round_pair(0)
         for d in range(D):
             gather(0, d)
         round_pair(1)
 
-        w_own = [keep.tile([P, N * PACK], BF16, name="w_bf%d" % d, align_bytes=64) for d in (1, 3)]
-        w_grouped = [picked[2][:, 1, :], w_own[0][:], picked[3][:, 1, :], w_own[1][:]]
+        w_own = keep.tile([P, N * PACK], BF16, name="w_bf2", align_bytes=64)
+        w_grouped = [picked[2][:, 1, :], picked[3][:, 1, :], w_own[:]]
 
-        WIDE_COPY = [nc.vector.tensor_copy, nc.vector.tensor_copy, nc.vector.tensor_copy]
         gather(1, 0)
         gather(1, 1)
         for d in range(D - 1):
             quantize_w(d, w_grouped[d])
-            grouped = keep.tile([P, 512 * PACK], BF16, name="wide_bf%d" % d, tag="wide_bf%d" % d, align_bytes=64)
-            x_mx = tokens("wide_x%d" % d, [(d, 0, 512)], grouped[:], WIDE_COPY[d], ["w_raw0", "wide_bf0", "w_raw2"][d])
+            grouped = keep.tile([P, 512 * PACK], BF16, name="wide_bf%d" % d, tag="w_raw2" if d == 2 else "", align_bytes=64)
+            copy = nc.scalar.copy if d == 2 else nc.vector.tensor_copy
+            x_mx = tokens("wide_x%d" % d, [(d, 0, 512)], grouped[:], copy, ["w_raw0", "w_raw1", ""][d])
             for c in range(BLOCKS):
                 product(wide[c][:], d, c, x_mx, slice(0, 512), d == 0, False)
-            if d == 0:
-                gather(1, 2)
-        for c in range(WARM):
-            product(last[c % 2][:].rearrange("p i v -> p (i v)"), 2, c, x_mx, slice(0, 256), True, True)
-            product(mid[c % 2][:, 0, :], 2, c, x_mx, slice(256, 512), True, True)
-        gather(1, 3)
-        round_w(3, w_grouped[3])
-        chain = [w_grouped[3][:, 0 : 256 * PACK], w_grouped[3][:, 256 * PACK :]]
+            if d == 1:
+                for c in range(WARM):
+                    product(mid[c][:], d, c, x_mx, slice(0, 512), True, True)
+            if d < 2:
+                gather(1, d + 2)
+        chain = [picked[2][:, 0, 0 : 256 * PACK], picked[2][:, 1, 0 : 256 * PACK]]
+        for h in range(2):
+            nc.scalar.activation(
+                chain[h].rearrange("p (c i t) -> p c t i", i=RUN, t=PACK),
+                w_raw[3 + h][:].rearrange("p t (c i) -> p c t i", i=RUN),
+                ACT.Copy,
+            )
         front = quantize("w3_front", chain[0], 256)
-        half = keep.tile([P, 256 * PACK], BF16, name="half_bf", tag="w_raw3", align_bytes=64)
+        half = keep.tile([P, 256 * PACK], BF16, name="half_bf", tag="w_raw3_0", align_bytes=64)
         x_halves = [tokens("wide_x3_0", [(3, 0, 256)], half[:]), tokens("wide_x3_1", [(3, 256, 512)], chain[0])]
-        back = quantize("w3_back", chain[1], 256, "w_raw3")
+        back = quantize("w3_back", chain[1], 256, "w_raw3_0")
         for c in range(BLOCKS):
             codes, scales = (front, back)[c // 2]
             cols = slice(c % 2 * P, (c % 2 + 1) * P)
@@ -174,23 +181,19 @@ def tile_picked_merge_lin_silu_sub_e_kernel(tc, xT, w, b, offs, out):
         for d in range(D):
             x_mx = tokens("mid_x%d" % d, [(d, 512, 768)], chain[d % 2])
             for c in range(BLOCKS):
-                product(mid[c // 2][:, c % 2, :], d, c, x_mx, slice(0, 256), d == 0 and c % 2 == 0, d == D - 1 and c % 2 == 1)
-        for j in range(2):
-            y = keep.tile([P, 2, 256], F32, name="y_mid%d" % j)
-            for i in range(2):
-                c = 2 * j + i
-                nc.scalar.activation(y[:, i, :], mid[j][:, i, :], ACT.Silu, bias=bias[:, c : c + 1])
-            nc.sync.dma_start(out=out_blocks[:, 2 * j : 2 * j + 2, 512:768], in_=y[:])
+                product(mid[c][:, 0:256], d, c, x_mx, slice(0, 256), d == 0, d == D - 1)
+        for c in range(BLOCKS):
+            y = keep.tile([P, 256], F32, name="y_mid%d" % c)
+            nc.scalar.activation(y[:], mid[c][:, 0:256], ACT.Silu, bias=bias[:, c : c + 1])
+            nc.sync.dma_start(out=out_blocks[:, c, 512:768], in_=y[:])
 
         for h in range(2):
             x_mx = tokens("last_x%d" % h, [(2 * h, 768, V), (2 * h + 1, 768, V)], chain[h])
             for c in range(BLOCKS):
                 for i in range(2):
                     d = 2 * h + i
-                    product(last[c // 2][:, c % 2, :], d, c, x_mx, slice(128 * i, 128 * i + 128), d == 0 and c % 2 == 0, d == D - 1 and c % 2 == 1)
-        for j in range(2):
-            y = keep.tile([P, 2, 128], F32, name="y_last%d" % j)
-            for i in range(2):
-                c = 2 * j + i
-                nc.scalar.activation(y[:, i, :], last[j][:, i, :], ACT.Silu, bias=bias[:, c : c + 1])
-            nc.sync.dma_start(out=out_blocks[:, 2 * j : 2 * j + 2, 768:V], in_=y[:])
+                    product(wide[c][:, 0:128], d, c, x_mx, slice(128 * i, 128 * i + 128), d == 0, d == D - 1)
+        for c in range(BLOCKS):
+            y = keep.tile([P, 128], F32, name="y_last%d" % c)
+            nc.scalar.activation(y[:], wide[c][:, 0:128], ACT.Silu, bias=bias[:, c : c + 1])
+            nc.sync.dma_start(out=out_blocks[:, c, 768:V], in_=y[:])

from contextlib import ExitStack

import concourse.mybir as mybir

K, T, D, S, V, N = 512, 4096, 4, 3584, 896, 512
FLOPS = 2 * K * S * N

F32 = mybir.dt.float32
BF16 = mybir.dt.bfloat16
U32 = mybir.dt.uint32
U16 = mybir.dt.uint16
U8 = mybir.dt.uint8
FP8X4 = mybir.dt.float8_e4m3fn_x4
ACT = mybir.ActivationFunctionType

P = 128
PACK = 4
RUN = 4
LIST_ROWS = 16
BLOCKS = N // P
WARM = 4

X_CHUNKS = [
    [(2048, 704), (1536, 512), (512, 160)],
    [(1024, 1024), (1024, 1024), (1024, 1024), (768, 256), (256, 0)],
]


def tile_picked_merge_lin_silu_sub_e_kernel(tc, xT, w, b, offs, out):
    nc = tc.nc
    with ExitStack() as ctx:
        keep = ctx.enter_context(tc.tile_pool(name="keep", bufs=1))
        psum = ctx.enter_context(tc.psum_pool(name="psum", bufs=1))

        offsets = keep.tile([P, S // LIST_ROWS], U16, name="offsets")
        bias = keep.tile([P, BLOCKS], F32, name="bias")

        warm_in = keep.tile([P, 8], F32, name="warm_in")
        warm_out = keep.tile([P, 8], F32, name="warm_out")
        nc.vector.memset(warm_in[:], 0.0)
        nc.scalar.activation(warm_out[:], warm_in[:], ACT.Silu)

        x_rows = xT.rearrange("(p t) c -> p t c", t=PACK)
        x_raw = [[], []]
        for u in range(2):
            first = 0
            for i, (width, share) in enumerate(X_CHUNKS[u]):
                raw = keep.tile([P, 2, width], F32, name="x_raw%d_%d" % (u, i))
                nc.sync.dma_start(out=raw[:], in_=x_rows[:, 2 * u : 2 * u + 2, first : first + width])
                x_raw[u].append(raw)
                first += width
            if u == 0:
                nc.sync.dma_start(offsets[:], offs)
        w_raw = []
        for d in range(D - 1):
            raw = keep.tile([P, PACK, N], F32, name="w_raw%d" % d, tag="w_raw%d" % d, align_bytes=64)
            nc.sync.dma_start(out=raw[:], in_=w[d].rearrange("(p t) m -> p t m", t=PACK))
            w_raw.append(raw)
        for h in range(2):
            raw = keep.tile([P, PACK, 256], F32, name="w_raw3_%d" % h, tag="w_raw3_%d" % h, align_bytes=64)
            nc.sync.dma_start(out=raw[:], in_=w[3].rearrange("(p t) m -> p t m", t=PACK)[:, :, 256 * h : 256 * h + 256])
            w_raw.append(raw)
        with nc.allow_non_contiguous_dma(reason="one bias value a partition and block"):
            nc.sync.dma_start(out=bias[:], in_=b.rearrange("(c p) o -> p (c o)", p=P))

        pairs = [keep.tile([P, T, 2], BF16, name="pairs%d" % u, align_bytes=64) for u in range(2)]
        picked = [keep.tile([P, 2, N * PACK], BF16, name="picked%d" % d, align_bytes=64) for d in range(D)]

        def round_pair(u):
            first = 0
            for i, (width, share) in enumerate(X_CHUNKS[u]):
                src = x_raw[u][i][:].rearrange("p e (c i) -> p c e i", i=RUN)
                dst = pairs[u][:, first : first + width, :].rearrange("p (c i) e -> p c e i", i=RUN)
                cut = share // RUN
                if share > 0:
                    nc.scalar.activation(dst[:, :cut], src[:, :cut], ACT.Copy)
                if share < width:
                    nc.vector.tensor_copy(dst[:, cut:], src[:, cut:])
                first += width

        def gather(u, d):
            window = pairs[u][:].rearrange("p c e -> p (c e)").bitcast(U32)
            entries = offsets[:, d * V // LIST_ROWS : (d + 1) * V // LIST_ROWS]
            nc.vector.tensor_copy(picked[d][:, u, 0 : 2 * V].bitcast(U32), window.indirect(entries))

        def interleave(copy, dst, d, lo, hi):
            copy(
                dst.rearrange("p (c i) (u e) -> p c u i e", i=2, e=2),
                picked[d][:, :, 2 * lo : 2 * hi].rearrange("p u (c i e) -> p c u i e", i=2, e=2),
            )

        def quantize(name, grouped, width, codes_tag=""):
            codes = keep.tile([P, width], U32, name=name + "_codes", tag=codes_tag, align_bytes=64)
            scales = keep.tile([P, width], U8, name=name + "_scales", align_bytes=64)
            nc.vector.quantize_mx(out=codes[:].bitcast(FP8X4), scales=scales[:], in_=grouped)
            return codes, scales

        w_mx = {}

        def round_w(d, grouped):
            nc.scalar.activation(
                grouped.rearrange("p (c i t) -> p c t i", i=RUN, t=PACK),
                w_raw[d][:].rearrange("p t (c i) -> p c t i", i=RUN),
                ACT.Copy,
            )

        def quantize_w(d, grouped):
            round_w(d, grouped)
            codes, scales = quantize("w%d" % d, grouped, N)
            for c in range(BLOCKS):
                w_mx[d, c] = (codes[:, c * P : (c + 1) * P], scales[:, c * P : (c + 1) * P])

        def product(acc, d, c, x_mx, cols, start, stop):
            nc.tensor.matmul_mx(
                out=acc,
                lhsT=w_mx[d, c][0].bitcast(FP8X4),
                lhsT_scale=w_mx[d, c][1],
                rhs=x_mx[0][:, cols].bitcast(FP8X4),
                rhs_scale=x_mx[1][:, cols],
                start=start,
                stop=stop,
            )

        def tokens(name, pieces, grouped, copy=nc.vector.tensor_copy, codes_tag=""):
            first = 0
            for d, lo, hi in pieces:
                dst = grouped[:, first * PACK : (first + hi - lo) * PACK]
                interleave(copy, dst.rearrange("p (c t) -> p c t", t=PACK), d, lo, hi)
                first += hi - lo
            return quantize(name, grouped, first, codes_tag)

        out_blocks = out.rearrange("(c p) v -> p c v", p=P)
        wide = [psum.tile([P, 512], F32, name="wide%d" % c) for c in range(BLOCKS)]
        mid = [psum.tile([P, 512], F32, name="mid%d" % c) for c in range(BLOCKS)]

        round_pair(0)
        for d in range(D):
            gather(0, d)
        round_pair(1)

        w_own = keep.tile([P, N * PACK], BF16, name="w_bf2", align_bytes=64)
        w_grouped = [picked[2][:, 1, :], picked[3][:, 1, :], w_own[:]]

        gather(1, 0)
        gather(1, 1)
        for d in range(D - 1):
            quantize_w(d, w_grouped[d])
            grouped = keep.tile([P, 512 * PACK], BF16, name="wide_bf%d" % d, tag="w_raw2" if d == 2 else "", align_bytes=64)
            copy = nc.scalar.copy if d == 2 else nc.vector.tensor_copy
            x_mx = tokens("wide_x%d" % d, [(d, 0, 512)], grouped[:], copy, ["w_raw0", "w_raw1", ""][d])
            for c in range(BLOCKS):
                product(wide[c][:], d, c, x_mx, slice(0, 512), d == 0, False)
            if d == 1:
                for c in range(WARM):
                    product(mid[c][:], d, c, x_mx, slice(0, 512), True, True)
            if d < 2:
                gather(1, d + 2)
        chain = [picked[2][:, 0, 0 : 256 * PACK], picked[2][:, 1, 0 : 256 * PACK]]
        for h in range(2):
            nc.scalar.activation(
                chain[h].rearrange("p (c i t) -> p c t i", i=RUN, t=PACK),
                w_raw[3 + h][:].rearrange("p t (c i) -> p c t i", i=RUN),
                ACT.Copy,
            )
        front = quantize("w3_front", chain[0], 256)
        half = keep.tile([P, 256 * PACK], BF16, name="half_bf", tag="w_raw3_0", align_bytes=64)
        x_halves = [tokens("wide_x3_0", [(3, 0, 256)], half[:]), tokens("wide_x3_1", [(3, 256, 512)], chain[0])]
        back = quantize("w3_back", chain[1], 256, "w_raw3_0")
        for c in range(BLOCKS):
            codes, scales = (front, back)[c // 2]
            cols = slice(c % 2 * P, (c % 2 + 1) * P)
            w_mx[3, c] = (codes[:, cols], scales[:, cols])
        for c in range(BLOCKS):
            for h in range(2):
                product(wide[c][:, 256 * h : 256 * h + 256], 3, c, x_halves[h], slice(0, 256), False, h == 1)
        for c in range(BLOCKS):
            y = keep.tile([P, 512], F32, name="y_wide%d" % c)
            nc.scalar.activation(y[:], wide[c][:], ACT.Silu, bias=bias[:, c : c + 1])
            nc.sync.dma_start(out=out_blocks[:, c, 0:512], in_=y[:])

        for d in range(D):
            x_mx = tokens("mid_x%d" % d, [(d, 512, 768)], chain[d % 2])
            for c in range(BLOCKS):
                product(mid[c][:, 0:256], d, c, x_mx, slice(0, 256), d == 0, d == D - 1)
        for c in range(BLOCKS):
            y = keep.tile([P, 256], F32, name="y_mid%d" % c)
            nc.scalar.activation(y[:], mid[c][:, 0:256], ACT.Silu, bias=bias[:, c : c + 1])
            nc.sync.dma_start(out=out_blocks[:, c, 512:768], in_=y[:])

        for h in range(2):
            x_mx = tokens("last_x%d" % h, [(2 * h, 768, V), (2 * h + 1, 768, V)], chain[h])
            for c in range(BLOCKS):
                for i in range(2):
                    d = 2 * h + i
                    product(wide[c][:, 0:128], d, c, x_mx, slice(128 * i, 128 * i + 128), d == 0, d == D - 1)
        for c in range(BLOCKS):
            y = keep.tile([P, 128], F32, name="y_last%d" % c)
            nc.scalar.activation(y[:], wide[c][:, 0:128], ACT.Silu, bias=bias[:, c : c + 1])
            nc.sync.dma_start(out=out_blocks[:, c, 768:V], in_=y[:])
